import numpy as np
import ml_dtypes


def mxq(x, axis, fmt="e4m3"):
    dtype, down = {"e4m3": (ml_dtypes.float8_e4m3fn, 7), "e5m2": (ml_dtypes.float8_e5m2, 14)}[fmt]
    v = np.moveaxis(np.asarray(x, np.float32).astype(ml_dtypes.bfloat16).astype(np.float64), axis, -1)
    blocks = v.reshape(v.shape[:-1] + (-1, 32))
    amax = np.abs(blocks).max(-1, keepdims=True)
    byte = np.maximum(np.where(amax > 0, np.frexp(amax)[1] - 1 + 127, 0) - down, 1)
    scale = np.exp2(byte - 127.0)
    codes = (blocks / scale).astype(np.float32).astype(dtype).astype(np.float64)
    return np.moveaxis((codes * scale).reshape(v.shape), -1, axis)


WIDE = False


def mx_kscale(k, group=512):
    if not WIDE:
        return np.ones(k)
    levels = np.array([18, -18])
    if group != 512:
        return np.exp2(np.random.permutation(np.resize(levels, k // group))).repeat(group)
    if k % 512:
        return np.exp2(np.random.permutation(np.resize(levels, k // 32))).repeat(32)
    a = np.empty((k // 512, 16))
    for p in range(k // 512):
        a[p, :8] = np.random.permutation(np.resize(levels, 8))
        for g in range(8):
            far = levels[np.abs(levels - a[p, g]) >= 10]
            a[p, g + 8] = far[np.random.randint(len(far))]
    return np.exp2(a.ravel()).repeat(32)


def f64(x):
    return np.asarray(x).astype(np.float64)


def bf(x):
    return np.asarray(x, np.float32).astype(ml_dtypes.bfloat16)


def planes(Y):
    r, m = Y.shape
    b = f64(bf(Y)).reshape(r // 32, 32, m)
    amax = np.abs(b).max(1)
    byte = np.clip(np.where(amax > 0, np.frexp(amax)[1] - 1 + 127 - 7, 1), 1, 254)
    codes = (b * np.exp2(127.0 - byte)[:, None, :]).reshape(r, m).astype(np.float32).astype(ml_dtypes.float8_e4m3fn).view(np.uint8)
    words = codes.reshape(r // 512, 128, 4, m).transpose(0, 1, 3, 2)
    return np.ascontiguousarray(words), np.ascontiguousarray(byte.astype(np.uint8).reshape(r // 512, 16, m))


G, D, M, N = 4, 128, 128, 512


def setup_inputs():
    n = np.random.standard_normal
    s_d = mx_kscale(D, 0)
    return {
        "h": (n((G, D, N)) * s_d[:, None]).astype(np.float32),
        "ws": (n((G, D, M)) / np.sqrt(D) / s_d[:, None]).astype(np.float32),
        "y0": (n((G, M, N))).astype(np.float32),
        "sh": (n((G, M, N))).astype(np.float32),
    }


def reference(h, ws, y0, sh):
    wsq = mxq(f64(ws), 1, "e4m3")
    hq = mxq(f64(h), 1, "e4m3")
    zs = wsq.transpose(0, 2, 1) @ hq
    y = f64(y0) * (1.0 + np.tanh(zs)) + f64(sh)
    Y = y.reshape(G * M, N)
    words, scales = planes(Y)
    return Y, words, scales

from contextlib import ExitStack

import concourse.mybir as mybir

G, D, M, N = 4, 128, 128, 512
FLOPS = 2 * G * D * M * N

F32 = mybir.dt.float32
BF16 = mybir.dt.bfloat16
I32 = mybir.dt.int32
U32 = mybir.dt.uint32
U8 = mybir.dt.uint8
FP8X4 = mybir.dt.float8_e4m3fn_x4
ALU = mybir.AluOpType
ACT = mybir.ActivationFunctionType

P = 128
PACK = 4
ROWS = D // PACK
HALF = N // 2
MM_N = 128
VECTOR_COLS = 160


def interleave(copy, dst, src):
    copy(out=dst.rearrange("p (c i) t -> p c t i", i=4), in_=src.rearrange("p t (c i) -> p c t i", i=4))


def quantize(nc, codes, scales, packed):
    nc.vector.quantize_mx(out=codes.bitcast(FP8X4), scales=scales, in_=packed.rearrange("p c t -> p (c t)"))


def tile_rows_pl_cell_film_kernel(tc, h, ws, y0, sh, out_0, out_1, out_2):
    nc = tc.nc
    halves = [slice(u * HALF, (u + 1) * HALF) for u in range(2)]

    with ExitStack() as ctx:
        sb = ctx.enter_context(tc.tile_pool(name="sb", bufs=1))
        ps = ctx.enter_context(tc.psum_pool(name="ps", bufs=1))
        ctx.enter_context(tc.manual_schedule())

        def tiles(pool, name, count, shape, dtype):
            return [pool.tile(shape, dtype, name="%s%d" % (name, i), align_bytes=64) for i in range(count)]

        ws_raw = sb.tile([P, PACK, M], F32, align_bytes=64)
        ws_packed = sb.tile([P, M, PACK], BF16, align_bytes=64)
        ws_codes = sb.tile([P, M], U32, align_bytes=64)
        ws_scales = sb.tile([P, M], U8, align_bytes=64)
        h_raw = tiles(sb, "h_raw", 2, [P, PACK, HALF], F32)
        h_packed = tiles(sb, "h_packed", 2, [P, HALF, PACK], BF16)
        h_codes = tiles(sb, "h_codes", 2, [P, HALF], U32)
        h_scales = tiles(sb, "h_scales", 2, [P, HALF], U8)
        y0_sb = tiles(sb, "y0_sb", G, [P, N], F32)
        sh_sb = tiles(sb, "sh_sb", G, [P, N], F32)
        gate = tiles(sb, "gate", G, [P, N], F32)
        scaled = tiles(sb, "scaled", G, [P, N], F32)
        y = tiles(sb, "y", G, [P, N], F32)
        y_bf = tiles(sb, "y_bf", G, [P, N], BF16)
        y_rows = tiles(sb, "y_rows", 2, [P, PACK, HALF], BF16)
        y_packed = tiles(sb, "y_packed", 2, [P, HALF, PACK], BF16)
        y_codes = tiles(sb, "y_codes", 2, [P, HALF], U32)
        y_scales = sb.tile([P, 2, HALF], U8, align_bytes=64)
        zs = [[ps.tile([P, HALF], F32, name="zs%d_%d" % (g, u)) for u in range(2)] for g in range(G)]

        h_rows = h.rearrange("g (p j) n -> (g p) j n", j=PACK)
        words_out = out_1.rearrange("v p n t -> (v p) (n t)").bitcast(I32)
        scales_out = out_2.bitcast(I32).rearrange("v (r s b) (u n) -> u s (v b) r n", r=2, s=2, u=2)

        nc.sync.dma_start(out=ws_raw[:], in_=ws.rearrange("g (p j) m -> (g p) j m", j=PACK))
        for u in range(2):
            nc.sync.dma_start(out=h_raw[u][:], in_=h_rows[:, :, halves[u]])
        for src, dst, g in [(y0, y0_sb, 0), (y0, y0_sb, 1), (sh, sh_sb, 0), (sh, sh_sb, 1),
                            (y0, y0_sb, 2), (sh, sh_sb, 2), (y0, y0_sb, 3), (sh, sh_sb, 3)]:
            nc.sync.dma_start(out=dst[g][:], in_=src[g])

        def pack_shared(dst, src):
            interleave(nc.vector.tensor_copy, dst[:, :VECTOR_COLS, :], src[:, :, :VECTOR_COLS])
            interleave(nc.scalar.copy, dst[:, VECTOR_COLS:, :], src[:, :, VECTOR_COLS:])

        def product(g, u):
            rows = slice(ROWS * g, ROWS * (g + 1))
            for c0 in range(0, HALF, MM_N):
                cols = slice(c0, c0 + MM_N)
                nc.tensor.matmul_mx(
                    out=zs[g][u][:, cols],
                    lhsT=ws_codes[rows, :].bitcast(FP8X4),
                    lhsT_scale=ws_scales[rows, :],
                    rhs=h_codes[u][rows, cols].bitcast(FP8X4),
                    rhs_scale=h_scales[u][rows, cols],
                    start=True,
                    stop=True,
                )

        interleave(nc.vector.tensor_copy, ws_packed[:], ws_raw[:])
        quantize(nc, ws_codes[:], ws_scales[:], ws_packed[:])
        for u in range(2):
            pack_shared(h_packed[u], h_raw[u])
            quantize(nc, h_codes[u][:], h_scales[u][:], h_packed[u][:])
            for g in range(G):
                product(g, u)

        for u in range(2):
            for g in range(G):
                nc.scalar.activation(out=gate[g][:, halves[u]], in_=zs[g][u][:], func=ACT.Tanh)

        def modulate(g, u):
            nc.vector.scalar_tensor_tensor(
                out=scaled[g][:, halves[u]], in0=gate[g][:, halves[u]], scalar=1.0, in1=y0_sb[g][:, halves[u]],
                op0=ALU.add, op1=ALU.mult,
            )

        def shift(dst, g, u):
            nc.vector.tensor_tensor(out=dst[g][:, halves[u]], in0=scaled[g][:, halves[u]], in1=sh_sb[g][:, halves[u]], op=ALU.add)

        def regroup(g, u):
            first = 64 * u + ROWS * (g % 2)
            nc.sync.dma_start(out=y_rows[g // 2][first : first + ROWS, :, :], in_=y_bf[g][:, halves[u]])

        def store_y(g):
            nc.sync.dma_start(out=out_0[M * g : M * (g + 1), :], in_=y[g][:])

        def finish(g, u):
            if g == G - 1:
                shift(y_bf, g, u)
            else:
                shift(y, g, u)
                nc.scalar.copy(out=y_bf[g][:, halves[u]], in_=y[g][:, halves[u]])
            regroup(g, u)

        def store_words(pair, queues):
            for u in range(2):
                queues[u].dma_start(
                    out=words_out[64 * pair : 64 * (pair + 1), halves[u]],
                    in_=y_codes[pair][64 * u : 64 * (u + 1), :].bitcast(I32),
                )

        units = [(0, 0), (1, 0), (0, 1), (1, 1), (2, 0), (2, 1), (3, 0), (3, 1)]
        for i, (g, u) in enumerate(units):
            modulate(g, u)
            if i > 0:
                finish(*units[i - 1])
            if (g, u) == (2, 0):
                store_y(0)
        finish(*units[-1])
        store_y(1)
        store_y(2)

        interleave(nc.vector.tensor_copy, y_packed[0][:], y_rows[0][:])
        for u in range(2):
            shift(y, G - 1, u)
        quantize(nc, y_codes[0][:], y_scales[:, 0, :], y_packed[0][:])
        store_y(G - 1)
        store_words(0, [nc.sync, nc.sync])

        pack_shared(y_packed[1], y_rows[1])
        quantize(nc, y_codes[1][:], y_scales[:, 1, :], y_packed[1][:])
        store_words(1, [nc.sync, nc.scalar])
        scale_words = y_scales[:].bitcast(I32)
        for u in range(2):
            for s in range(2):
                first = 64 * u + ROWS * s
                [nc.sync, nc.scalar][s].dma_start(out=scales_out[u, s], in_=scale_words[first : first + 4, :, :])
